import numpy as np
import ml_dtypes


def mxq(x, axis, fmt="e4m3"):
    dtype, down = {"e4m3": (ml_dtypes.float8_e4m3fn, 7), "e5m2": (ml_dtypes.float8_e5m2, 14)}[fmt]
    v = np.moveaxis(np.asarray(x, np.float32).astype(ml_dtypes.bfloat16).astype(np.float64), axis, -1)
    blocks = v.reshape(v.shape[:-1] + (-1, 32))
    amax = np.abs(blocks).max(-1, keepdims=True)
    byte = np.maximum(np.where(amax > 0, np.frexp(amax)[1] - 1 + 127, 0) - down, 1)
    scale = np.exp2(byte - 127.0)
    codes = (blocks / scale).astype(np.float32).astype(dtype).astype(np.float64)
    return np.moveaxis((codes * scale).reshape(v.shape), -1, axis)


WIDE = False


def mx_kscale(k):
    if not WIDE:
        return np.ones(k)
    levels = np.array([30, -30])
    if k % 512:
        return np.exp2(np.random.permutation(np.resize(levels, k // 32))).repeat(32)
    a = np.empty((k // 512, 16))
    for p in range(k // 512):
        a[p, :8] = np.random.permutation(np.resize(levels, 8))
        for g in range(8):
            far = levels[np.abs(levels - a[p, g]) >= 10]
            a[p, g + 8] = far[np.random.randint(len(far))]
    return np.exp2(a.ravel()).repeat(32)


def f64(x):
    return np.asarray(x).astype(np.float64)


def striped(idx):
    return np.tile(np.asarray(idx).reshape(-1, 16).T, (8, 1)).astype(np.uint16)


def unstriped(offs):
    return offs[:16].T.reshape(-1).astype(np.int64)


E2M1 = np.array([0.0, 0.5, 1.0, 1.5, 2.0, 3.0, 4.0, 6.0, -0.0, -0.5, -1.0, -1.5, -2.0, -3.0, -4.0, -6.0])


def pack_weight(w, fmt):
    k, n = w.shape
    w = f64(np.asarray(w, np.float32).astype(ml_dtypes.bfloat16)).reshape(k // 32, 32, n)
    amax = np.abs(w).max(1)
    if fmt in ("e4m3", "e5m2"):
        byte = np.frexp(amax)[1] - 1 + 127 - (7 if fmt == "e4m3" else 14)
    else:
        mant, ex = np.frexp(amax / 6.0)
        byte = np.where(mant > 0.5, ex, ex - 1) + 127
    byte = np.clip(np.where(amax > 0, byte, 1), 1, 254)
    scaled = (w * np.exp2(127.0 - byte)[:, None, :]).reshape(k, n).astype(np.float32)
    by_word = np.ascontiguousarray(scaled.reshape(k // 512, 128, 4, n).transpose(0, 1, 3, 2))
    if fmt in ("e4m3", "e5m2"):
        words = by_word.astype(ml_dtypes.float8_e4m3fn if fmt == "e4m3" else ml_dtypes.float8_e5m2).view(np.uint8)
    else:
        c = by_word.astype(ml_dtypes.float4_e2m1fn).view(np.uint8) & 0xF
        words = (c[..., 0::2] | (c[..., 1::2] << 4)).reshape(k // 512, 128, 2 * n)
    return np.ascontiguousarray(words), np.ascontiguousarray(byte.astype(np.uint8).reshape(k // 512, 16, n))


def unpack_weight(words, scales, fmt):
    g, _, n = scales.shape
    words = np.ascontiguousarray(words).reshape(g, 128, n, -1)
    if fmt in ("e4m3", "e5m2"):
        vals = words.view(ml_dtypes.float8_e4m3fn if fmt == "e4m3" else ml_dtypes.float8_e5m2).astype(np.float64)
    else:
        nib = np.empty((g, 128, n, 4), np.uint8)
        nib[..., 0::2] = words & 0xF
        nib[..., 1::2] = words >> 4
        vals = E2M1[nib]
    vals = vals * np.repeat(np.exp2(scales.astype(np.float64) - 127.0), 8, axis=1)[..., None]
    return vals.transpose(0, 1, 3, 2).reshape(g * 512, n)


def sigmoid(v):
    return 1.0 / (1.0 + np.exp(-v))


K, T, J, R, C, N = 512, 512, 256, 512, 1024, 256


def setup_inputs():
    n = np.random.standard_normal
    idx = np.random.permutation(T)[:J]
    idx2 = np.random.permutation(T)[:J]
    idx3 = np.random.permutation(C)[:R]
    fk = mx_kscale(K)
    fr = mx_kscale(R)
    wp = pack_weight(n((K, R)) * 1 / np.sqrt(K) * fk[:, None], "e5m2")
    wbp = pack_weight(n((R, N)) * 1 / np.sqrt(R) / fr[:, None], "e4m3")
    return {
        "xf": (n((K, T))).astype(np.float32),
        "fk": (np.random.uniform(0.5, 2.0, (K, 1)) / fk[:, None]).astype(np.float32),
        "w_words": wp[0],
        "w_scales": wp[1],
        "us": (np.random.uniform(0.5, 1.5, (1, R)) * fr).astype(np.float32),
        "tg": (1.0 * n((J, C))).astype(np.float32),
        "wb_words": wbp[0],
        "wb_scales": wbp[1],
        "rs": (1.0 * n((J, N))).astype(np.float32),
        "offs": striped(idx),
        "offs2": striped(idx2),
        "offs3": striped(idx3),
    }


def reference(xf, fk, w_words, w_scales, us, tg, wb_words, wb_scales, rs, offs, offs2, offs3):
    idx = unstriped(offs)
    idx2 = unstriped(offs2)
    idx3 = unstriped(offs3)
    wu = unpack_weight(w_words, w_scales, "e5m2")
    wbu = unpack_weight(wb_words, wb_scales, "e4m3")
    u = np.maximum(f64(xf)[:, idx], f64(xf)[:, idx2]) * f64(fk)
    uq = mxq(u, 0, "e5m2")
    a = uq.T @ wu
    hr = a * sigmoid(f64(tg)[:, idx3]) * f64(us)
    hid = hr.T
    hidq = mxq(hid, 0, "e5m2")
    p = hidq.T @ wbu
    pk2 = np.max(np.abs(p), axis=1, keepdims=True)
    y = p / (pk2 + 0.2) + 0.3 * f64(rs)
    return y

@@ -1,0 +1,166 @@
+from contextlib import ExitStack
+
+import concourse.mybir as mybir
+from concourse.masks import make_identity
+
+K, T, J, R, C, N = 512, 512, 256, 512, 1024, 256
+FLOPS = 2 * J * K * R + 2 * J * R * N
+
+F32 = mybir.dt.float32
+BF16 = mybir.dt.bfloat16
+I32 = mybir.dt.int32
+U32 = mybir.dt.uint32
+U16 = mybir.dt.uint16
+U8 = mybir.dt.uint8
+E5M2X4 = mybir.dt.float8_e5m2_x4
+E4M3X4 = mybir.dt.float8_e4m3fn_x4
+ALU = mybir.AluOpType
+ACT = mybir.ActivationFunctionType
+
+P = 128
+PACK = 4
+TILES = J // P
+LINE = 4
+
+
+def tile_list_rows_largerpicks_tabled_rowpeaks_kernel(
+    tc, xf, fk, w_words, w_scales, us, tg, wb_words, wb_scales, rs, offs, offs2, offs3, out
+):
+    nc = tc.nc
+    with ExitStack() as ctx:
+        sb = ctx.enter_context(tc.tile_pool(name="sb", bufs=1))
+        ps = ctx.enter_context(tc.psum_pool(name="ps", bufs=1))
+
+        def by_line(ap):
+            return ap.rearrange("p t (c i) -> p c t i", i=LINE)
+
+        def words_by_line(ap):
+            return ap.rearrange("p (c i) t -> p c t i", i=LINE)
+
+        list_a = sb.tile([P, J // 16], U16, name="list_a")
+        list_b = sb.tile([P, J // 16], U16, name="list_b")
+        list_g = sb.tile([P, R // 16], U16, name="list_g")
+        x_plane = [sb.tile([P, T], F32, name=f"x_plane{t}") for t in range(PACK)]
+        gate_in = [sb.tile([P, C], F32, name=f"gate_in{h}") for h in range(TILES)]
+        w_raw = sb.tile([P, R], U32, name="w_raw", align_bytes=64)
+        ws_raw = sb.tile([P, R], U8, name="ws_raw", align_bytes=64)
+        wb_sb = sb.tile([P, N], U32, name="wb_sb", align_bytes=64)
+        wbs_sb = sb.tile([P, N], U8, name="wbs_sb", align_bytes=64)
+        fk_sb = sb.tile([P, PACK], F32, name="fk_sb")
+        us_sb = sb.tile([P, PACK], F32, name="us_sb")
+        rs_sb = sb.tile([P, TILES, N], F32, name="rs_sb")
+        ident = sb.tile([P, P], F32, name="ident")
+
+        nc.vector.memset(ws_raw[:].bitcast(I32), 0)
+        nc.vector.memset(wbs_sb[:].bitcast(I32), 0)
+        make_identity(nc, ident[:])
+
+        xf_planes = xf.rearrange("(p t) c -> p t c", t=PACK)
+        nc.sync.dma_start(list_a[:], offs)
+        nc.sync.dma_start(x_plane[0][:], xf_planes[:, 0, :])
+        nc.sync.dma_start(list_g[:], offs3)
+        nc.sync.dma_start(gate_in[0][:], tg[0:P, :])
+        nc.sync.dma_start(list_b[:], offs2)
+        nc.sync.dma_start(x_plane[1][:], xf_planes[:, 1, :])
+        nc.sync.dma_start(x_plane[2][:], xf_planes[:, 2, :])
+        nc.sync.dma_start(x_plane[3][:], xf_planes[:, 3, :])
+        nc.sync.dma_start(gate_in[1][:], tg[P : 2 * P, :])
+        nc.sync.dma_start(w_raw[:].bitcast(I32), w_words[0].rearrange("p n t -> p (n t)").bitcast(I32))
+        nc.sync.dma_start(fk_sb[:], fk.rearrange("(p t) o -> p (t o)", t=PACK))
+        for q in range(4):
+            nc.sync.dma_start(ws_raw[32 * q : 32 * q + 4, :].bitcast(I32), w_scales[0, 4 * q : 4 * q + 4, :].bitcast(I32))
+        nc.sync.dma_start(us_sb[:], us.rearrange("o (p t) -> p (o t)", t=PACK))
+        nc.sync.dma_start(wb_sb[:].bitcast(I32), wb_words[0].rearrange("p n t -> p (n t)").bitcast(I32))
+        for q in range(4):
+            nc.sync.dma_start(wbs_sb[32 * q : 32 * q + 4, :].bitcast(I32), wb_scales[0, 4 * q : 4 * q + 4, :].bitcast(I32))
+        nc.sync.dma_start(rs_sb[:], rs.rearrange("(h p) n -> p h n", p=P))
+
+        pick_a = [sb.tile([P, J], F32, name=f"pick_a{t}") for t in range(PACK)]
+        pick_b = [sb.tile([P, J], F32, name=f"pick_b{t}") for t in range(PACK)]
+        larger = sb.tile([P, PACK, J], F32, name="larger")
+        gate = [sb.tile([P, R], F32, name=f"gate{h}") for h in range(TILES)]
+        gate_ps = [ps.tile([P, PACK, P], F32, name=f"gate_ps{h}") for h in range(TILES)]
+        gate_us = [sb.tile([P, PACK, P], F32, name=f"gate_us{h}") for h in range(TILES)]
+        w_sb = sb.tile([P, R], U32, name="w_sb", align_bytes=64)
+        ws_sb = sb.tile([P, R], U8, name="ws_sb", align_bytes=64)
+
+        def gate_gather(h):
+            nc.scalar.activation(gate[h][:], gate_in[h][:].indirect(list_g[:]), ACT.Sigmoid)
+            for t in range(PACK):
+                nc.tensor.transpose(gate_ps[h][:, t, :], gate[h][:, t::PACK], ident[:])
+
+        def gate_out(h):
+            for t in range(PACK):
+                nc.scalar.activation(gate_us[h][:, t, :], gate_ps[h][:, t, :], ACT.Copy, scale=us_sb[:, t : t + 1])
+
+        gate_gather(0)
+        for t in range(PACK):
+            nc.vector.tensor_copy(pick_a[t][:], x_plane[t][:].indirect(list_a[:]))
+            if t == 0:
+                nc.vector.tensor_copy(pick_b[t][:], x_plane[t][:].indirect(list_b[:]))
+            else:
+                nc.scalar.activation(pick_b[t][:], x_plane[t][:].indirect(list_b[:]), ACT.Copy)
+        for t in range(PACK):
+            nc.vector.tensor_tensor(larger[:, t, :], pick_a[t][:], pick_b[t][:], ALU.max)
+        gate_gather(1)
+        gate_out(0)
+        gate_out(1)
+
+        u_bf = [sb.tile([P, P, PACK], BF16, name=f"u_bf{h}", align_bytes=64) for h in range(TILES)]
+        u_q = [sb.tile([P, P], U32, name=f"u_q{h}", align_bytes=64) for h in range(TILES)]
+        u_s = [sb.tile([P, P], U8, name=f"u_s{h}", align_bytes=64) for h in range(TILES)]
+        fk_b = fk_sb[:].unsqueeze(1).unsqueeze(3).to_broadcast([P, P // LINE, PACK, LINE])
+        for h in range(TILES):
+            nc.vector.tensor_tensor(words_by_line(u_bf[h][:]), by_line(larger[:, :, h * P : (h + 1) * P]), fk_b, ALU.mult)
+        nc.vector.tensor_copy(
+            w_sb[:].bitcast(I32).rearrange("p (t m) -> p m t", t=PACK), w_raw[:].bitcast(I32).rearrange("p (m t) -> p m t", t=PACK)
+        )
+        nc.vector.tensor_copy(
+            ws_sb[:].rearrange("p (t m) -> p t m", t=PACK), ws_raw[:].rearrange("p (m t) -> p t m", t=PACK)
+        )
+        a_ps = [ps.tile([P, PACK, P], F32, name=f"a_ps{h}") for h in range(TILES)]
+        for h in range(TILES):
+            nc.vector.quantize_mx(u_q[h][:].bitcast(E5M2X4), u_s[h][:], u_bf[h][:].rearrange("p j t -> p (j t)"))
+            for t in range(PACK):
+                nc.tensor.matmul_mx(
+                    a_ps[h][:, t, :],
+                    lhsT=w_sb[:, t * P : (t + 1) * P].bitcast(E5M2X4),
+                    lhsT_scale=ws_sb[:, t * P : (t + 1) * P],
+                    rhs=u_q[h][:].bitcast(E5M2X4),
+                    rhs_scale=u_s[h][:],
+                    start=True,
+                    stop=True,
+                )
+
+        rs3 = sb.tile([P, TILES, N], F32, name="rs3")
+        nc.scalar.activation(rs3[:], rs_sb[:], ACT.Copy, scale=0.3)
+
+        h_bf = [sb.tile([P, P, PACK], BF16, name=f"h_bf{h}", align_bytes=64) for h in range(TILES)]
+        h_q = [sb.tile([P, P], U32, name=f"h_q{h}", align_bytes=64) for h in range(TILES)]
+        h_s = [sb.tile([P, P], U8, name=f"h_s{h}", align_bytes=64) for h in range(TILES)]
+        p_ps = [ps.tile([P, N], F32, name=f"p_ps{h}") for h in range(TILES)]
+        for h in range(TILES):
+            nc.vector.tensor_tensor(words_by_line(h_bf[h][:]), by_line(a_ps[h][:]), by_line(gate_us[h][:]), ALU.mult)
+        for h in range(TILES):
+            nc.vector.quantize_mx(h_q[h][:].bitcast(E5M2X4), h_s[h][:], h_bf[h][:].rearrange("p j t -> p (j t)"))
+            nc.tensor.matmul_mx(
+                p_ps[h][:],
+                lhsT=h_q[h][:].bitcast(E5M2X4),
+                lhsT_scale=h_s[h][:],
+                rhs=wb_sb[:].bitcast(E4M3X4),
+                rhs_scale=wbs_sb[:],
+                start=True,
+                stop=True,
+            )
+
+        mag = [sb.tile([P, N], F32, name=f"mag{h}") for h in range(TILES)]
+        mag_up = [sb.tile([P, N], F32, name=f"mag_up{h}") for h in range(TILES)]
+        den = [sb.tile([P, 1], F32, name=f"den{h}") for h in range(TILES)]
+        inv = [sb.tile([P, 1], F32, name=f"inv{h}") for h in range(TILES)]
+        res = [sb.tile([P, N], F32, name=f"res{h}") for h in range(TILES)]
+        for h in range(TILES):
+            nc.scalar.activation(mag[h][:], p_ps[h][:], ACT.Abs)
+            nc.vector.tensor_scalar(mag_up[h][:], mag[h][:], 0.2, None, ALU.add, ALU.max, accum_out=den[h][:])
+            nc.vector.reciprocal(inv[h][:], den[h][:])
+            nc.vector.scalar_tensor_tensor(res[h][:], p_ps[h][:], inv[h][:], rs3[:, h, :], ALU.mult, ALU.add)
+            nc.sync.dma_start(out[h * P : (h + 1) * P, :], res[h][:])

@@ -51,6 +51,10 @@ def tile_list_rows_largerpicks_tabled_rowpeaks_kernel(
         rs_sb = sb.tile([P, TILES, N], F32, name="rs_sb")
         ident = sb.tile([P, P], F32, name="ident")
 
+        warm_in = sb.tile([P, 1], F32, name="warm_in")
+        warm_out = sb.tile([P, 1], F32, name="warm_out")
+        nc.gpsimd.memset(warm_in[:], 0.0)
+        nc.scalar.activation(warm_out[:], warm_in[:], ACT.Sigmoid)
         nc.vector.memset(ws_raw[:].bitcast(I32), 0)
         nc.vector.memset(wbs_sb[:].bitcast(I32), 0)
         make_identity(nc, ident[:])

@@ -53,37 +53,41 @@ def tile_list_rows_largerpicks_tabled_rowpeaks_kernel(
 
         warm_in = sb.tile([P, 1], F32, name="warm_in")
         warm_out = sb.tile([P, 1], F32, name="warm_out")
-        nc.gpsimd.memset(warm_in[:], 0.0)
+        nc.gpsimd.memset(ws_raw[:].bitcast(I32), 0)
+        nc.vector.memset(warm_in[:], 0.0)
         nc.scalar.activation(warm_out[:], warm_in[:], ACT.Sigmoid)
-        nc.vector.memset(ws_raw[:].bitcast(I32), 0)
         nc.vector.memset(wbs_sb[:].bitcast(I32), 0)
-        make_identity(nc, ident[:])
+        nc.vector.memset(ident[:], 0.0)
+        make_identity(nc, ident[:], nomemset=True)
 
         xf_planes = xf.rearrange("(p t) c -> p t c", t=PACK)
-        nc.sync.dma_start(list_a[:], offs)
         nc.sync.dma_start(x_plane[0][:], xf_planes[:, 0, :])
+        nc.sync.dma_start(list_a[:], offs)
+        nc.sync.dma_start(list_b[:], offs2)
+        for t in range(1, PACK):
+            nc.sync.dma_start(x_plane[t][:], xf_planes[:, t, :])
         nc.sync.dma_start(list_g[:], offs3)
         nc.sync.dma_start(gate_in[0][:], tg[0:P, :])
-        nc.sync.dma_start(list_b[:], offs2)
-        nc.sync.dma_start(x_plane[1][:], xf_planes[:, 1, :])
-        nc.sync.dma_start(x_plane[2][:], xf_planes[:, 2, :])
-        nc.sync.dma_start(x_plane[3][:], xf_planes[:, 3, :])
-        nc.sync.dma_start(gate_in[1][:], tg[P : 2 * P, :])
-        nc.sync.dma_start(w_raw[:].bitcast(I32), w_words[0].rearrange("p n t -> p (n t)").bitcast(I32))
         nc.sync.dma_start(fk_sb[:], fk.rearrange("(p t) o -> p (t o)", t=PACK))
+        nc.sync.dma_start(gate_in[1][:], tg[P : 2 * P, :])
         for q in range(4):
-            nc.sync.dma_start(ws_raw[32 * q : 32 * q + 4, :].bitcast(I32), w_scales[0, 4 * q : 4 * q + 4, :].bitcast(I32))
+            nc.gpsimd.dma_start(ws_raw[32 * q : 32 * q + 4, :].bitcast(I32), w_scales[0, 4 * q : 4 * q + 4, :].bitcast(I32))
+        nc.sync.dma_start(w_raw[:].bitcast(I32), w_words[0].rearrange("p n t -> p (n t)").bitcast(I32))
         nc.sync.dma_start(us_sb[:], us.rearrange("o (p t) -> p (o t)", t=PACK))
         nc.sync.dma_start(wb_sb[:].bitcast(I32), wb_words[0].rearrange("p n t -> p (n t)").bitcast(I32))
         for q in range(4):
             nc.sync.dma_start(wbs_sb[32 * q : 32 * q + 4, :].bitcast(I32), wb_scales[0, 4 * q : 4 * q + 4, :].bitcast(I32))
         nc.sync.dma_start(rs_sb[:], rs.rearrange("(h p) n -> p h n", p=P))
 
-        pick_a = [sb.tile([P, J], F32, name=f"pick_a{t}") for t in range(PACK)]
-        pick_b = [sb.tile([P, J], F32, name=f"pick_b{t}") for t in range(PACK)]
+        pick_a = sb.tile([P, PACK, J], F32, name="pick_a")
+        pick_b = sb.tile([P, PACK, J], F32, name="pick_b")
         larger = sb.tile([P, PACK, J], F32, name="larger")
         gate = [sb.tile([P, R], F32, name=f"gate{h}") for h in range(TILES)]
-        gate_ps = [ps.tile([P, PACK, P], F32, name=f"gate_ps{h}") for h in range(TILES)]
+        first_bank = ps.tile([P, PACK, P], F32, name="first_bank", tag="first_bank")
+        gate_ps = [
+            [first_bank[:, t, :] for t in range(PACK)],
+            [ps.tile([P, P], F32, name=f"gate_ps{t}")[:] for t in range(PACK)],
+        ]
         gate_us = [sb.tile([P, PACK, P], F32, name=f"gate_us{h}") for h in range(TILES)]
         w_sb = sb.tile([P, R], U32, name="w_sb", align_bytes=64)
         ws_sb = sb.tile([P, R], U8, name="ws_sb", align_bytes=64)
@@ -91,21 +95,23 @@ def tile_list_rows_largerpicks_tabled_rowpeaks_kernel(
         def gate_gather(h):
             nc.scalar.activation(gate[h][:], gate_in[h][:].indirect(list_g[:]), ACT.Sigmoid)
             for t in range(PACK):
-                nc.tensor.transpose(gate_ps[h][:, t, :], gate[h][:, t::PACK], ident[:])
+                nc.tensor.transpose(gate_ps[h][t], gate[h][:, t::PACK], ident[:])
 
         def gate_out(h):
             for t in range(PACK):
-                nc.scalar.activation(gate_us[h][:, t, :], gate_ps[h][:, t, :], ACT.Copy, scale=us_sb[:, t : t + 1])
+                nc.scalar.activation(gate_us[h][:, t, :], gate_ps[h][t], ACT.Copy, scale=us_sb[:, t : t + 1])
 
-        gate_gather(0)
         for t in range(PACK):
-            nc.vector.tensor_copy(pick_a[t][:], x_plane[t][:].indirect(list_a[:]))
-            if t == 0:
-                nc.vector.tensor_copy(pick_b[t][:], x_plane[t][:].indirect(list_b[:]))
+            nc.scalar.activation(pick_b[:, t, :], x_plane[t][:].indirect(list_b[:]), ACT.Copy)
+            if t < PACK - 1:
+                nc.vector.tensor_copy(pick_a[:, t, :], x_plane[t][:].indirect(list_a[:]))
             else:
-                nc.scalar.activation(pick_b[t][:], x_plane[t][:].indirect(list_b[:]), ACT.Copy)
-        for t in range(PACK):
-            nc.vector.tensor_tensor(larger[:, t, :], pick_a[t][:], pick_b[t][:], ALU.max)
+                half = J // 2
+                nc.vector.tensor_copy(pick_a[:, t, :half], x_plane[t][:].indirect(list_a[:, : half // 16]))
+                nc.scalar.activation(pick_a[:, t, half:], x_plane[t][:].indirect(list_a[:, half // 16 :]), ACT.Copy)
+        for planes in (slice(0, 2), slice(2, 3), slice(3, 4)):
+            nc.vector.tensor_tensor(larger[:, planes, :], pick_a[:, planes, :], pick_b[:, planes, :], ALU.max)
+        gate_gather(0)
         gate_gather(1)
         gate_out(0)
         gate_out(1)
@@ -119,7 +125,7 @@ def tile_list_rows_largerpicks_tabled_rowpeaks_kernel(
         nc.vector.tensor_copy(
             w_sb[:].bitcast(I32).rearrange("p (t m) -> p m t", t=PACK), w_raw[:].bitcast(I32).rearrange("p (m t) -> p m t", t=PACK)
         )
-        nc.vector.tensor_copy(
+        nc.gpsimd.tensor_copy(
             ws_sb[:].rearrange("p (t m) -> p t m", t=PACK), ws_raw[:].rearrange("p (m t) -> p t m", t=PACK)
         )
         a_ps = [ps.tile([P, PACK, P], F32, name=f"a_ps{h}") for h in range(TILES)]
@@ -137,15 +143,14 @@ def tile_list_rows_largerpicks_tabled_rowpeaks_kernel(
                 )
 
         rs3 = sb.tile([P, TILES, N], F32, name="rs3")
-        nc.scalar.activation(rs3[:], rs_sb[:], ACT.Copy, scale=0.3)
+        nc.gpsimd.tensor_scalar(rs3[:], rs_sb[:], 0.3, 0.0, ALU.mult, ALU.add)
 
         h_bf = [sb.tile([P, P, PACK], BF16, name=f"h_bf{h}", align_bytes=64) for h in range(TILES)]
         h_q = [sb.tile([P, P], U32, name=f"h_q{h}", align_bytes=64) for h in range(TILES)]
         h_s = [sb.tile([P, P], U8, name=f"h_s{h}", align_bytes=64) for h in range(TILES)]
-        p_ps = [ps.tile([P, N], F32, name=f"p_ps{h}") for h in range(TILES)]
+        p_ps = [ps.tile([P, N], F32, name="p_ps0", tag="first_bank"), ps.tile([P, N], F32, name="p_ps1")]
         for h in range(TILES):
             nc.vector.tensor_tensor(words_by_line(h_bf[h][:]), by_line(a_ps[h][:]), by_line(gate_us[h][:]), ALU.mult)
-        for h in range(TILES):
             nc.vector.quantize_mx(h_q[h][:].bitcast(E5M2X4), h_s[h][:], h_bf[h][:].rearrange("p j t -> p (j t)"))
             nc.tensor.matmul_mx(
                 p_ps[h][:],

@@ -20,7 +20,7 @@ ACT = mybir.ActivationFunctionType
 P = 128
 PACK = 4
 TILES = J // P
-LINE = 4
+LINE = 2
 
 
 def tile_list_rows_largerpicks_tabled_rowpeaks_kernel(
@@ -74,10 +74,10 @@ def tile_list_rows_largerpicks_tabled_rowpeaks_kernel(
             nc.gpsimd.dma_start(ws_raw[32 * q : 32 * q + 4, :].bitcast(I32), w_scales[0, 4 * q : 4 * q + 4, :].bitcast(I32))
         nc.sync.dma_start(w_raw[:].bitcast(I32), w_words[0].rearrange("p n t -> p (n t)").bitcast(I32))
         nc.sync.dma_start(us_sb[:], us.rearrange("o (p t) -> p (o t)", t=PACK))
+        nc.sync.dma_start(rs_sb[:], rs.rearrange("(h p) n -> p h n", p=P))
         nc.sync.dma_start(wb_sb[:].bitcast(I32), wb_words[0].rearrange("p n t -> p (n t)").bitcast(I32))
         for q in range(4):
             nc.sync.dma_start(wbs_sb[32 * q : 32 * q + 4, :].bitcast(I32), wb_scales[0, 4 * q : 4 * q + 4, :].bitcast(I32))
-        nc.sync.dma_start(rs_sb[:], rs.rearrange("(h p) n -> p h n", p=P))
 
         pick_a = sb.tile([P, PACK, J], F32, name="pick_a")
         pick_b = sb.tile([P, PACK, J], F32, name="pick_b")
@@ -123,7 +123,8 @@ def tile_list_rows_largerpicks_tabled_rowpeaks_kernel(
         for h in range(TILES):
             nc.vector.tensor_tensor(words_by_line(u_bf[h][:]), by_line(larger[:, :, h * P : (h + 1) * P]), fk_b, ALU.mult)
         nc.vector.tensor_copy(
-            w_sb[:].bitcast(I32).rearrange("p (t m) -> p m t", t=PACK), w_raw[:].bitcast(I32).rearrange("p (m t) -> p m t", t=PACK)
+            w_sb[:].bitcast(I32).rearrange("p (t c i) -> p c t i", t=PACK, i=4),
+            w_raw[:].bitcast(I32).rearrange("p (c i t) -> p c t i", t=PACK, i=4),
         )
         nc.gpsimd.tensor_copy(
             ws_sb[:].rearrange("p (t m) -> p t m", t=PACK), ws_raw[:].rearrange("p (m t) -> p t m", t=PACK)
@@ -143,7 +144,7 @@ def tile_list_rows_largerpicks_tabled_rowpeaks_kernel(
                 )
 
         rs3 = sb.tile([P, TILES, N], F32, name="rs3")
-        nc.gpsimd.tensor_scalar(rs3[:], rs_sb[:], 0.3, 0.0, ALU.mult, ALU.add)
+        nc.scalar.activation(rs3[:], rs_sb[:], ACT.Copy, scale=0.3)
 
         h_bf = [sb.tile([P, P, PACK], BF16, name=f"h_bf{h}", align_bytes=64) for h in range(TILES)]
         h_q = [sb.tile([P, P], U32, name=f"h_q{h}", align_bytes=64) for h in range(TILES)]

@@ -19,8 +19,26 @@ ACT = mybir.ActivationFunctionType
 
 P = 128
 PACK = 4
-TILES = J // P
-LINE = 2
+SLOT_TILES = J // P
+LIST_ROWS = 16
+QUADRANTS = 4
+MX_ALIGN = 64
+PAIR = 2
+LINE_WORDS = 4
+SHARED_ENTRIES = J // 2
+
+
+def planes_by_pairs(planes):
+    return planes.rearrange("p t (c i) -> p c t i", i=PAIR)
+
+
+def words_by_pairs(words):
+    return words.rearrange("p (c i) t -> p c t i", i=PAIR)
+
+
+def load_scale_rows(nc, tile, scales):
+    for q in range(QUADRANTS):
+        nc.sync.dma_start(tile[32 * q : 32 * q + 4, :].bitcast(I32), scales[4 * q : 4 * q + 4, :].bitcast(I32))
 
 
 def tile_list_rows_largerpicks_tabled_rowpeaks_kernel(
@@ -31,24 +49,18 @@ def tile_list_rows_largerpicks_tabled_rowpeaks_kernel(
         sb = ctx.enter_context(tc.tile_pool(name="sb", bufs=1))
         ps = ctx.enter_context(tc.psum_pool(name="ps", bufs=1))
 
-        def by_line(ap):
-            return ap.rearrange("p t (c i) -> p c t i", i=LINE)
-
-        def words_by_line(ap):
-            return ap.rearrange("p (c i) t -> p c t i", i=LINE)
-
-        list_a = sb.tile([P, J // 16], U16, name="list_a")
-        list_b = sb.tile([P, J // 16], U16, name="list_b")
-        list_g = sb.tile([P, R // 16], U16, name="list_g")
+        list_a = sb.tile([P, J // LIST_ROWS], U16, name="list_a")
+        list_b = sb.tile([P, J // LIST_ROWS], U16, name="list_b")
+        list_g = sb.tile([P, R // LIST_ROWS], U16, name="list_g")
         x_plane = [sb.tile([P, T], F32, name=f"x_plane{t}") for t in range(PACK)]
-        gate_in = [sb.tile([P, C], F32, name=f"gate_in{h}") for h in range(TILES)]
-        w_raw = sb.tile([P, R], U32, name="w_raw", align_bytes=64)
-        ws_raw = sb.tile([P, R], U8, name="ws_raw", align_bytes=64)
-        wb_sb = sb.tile([P, N], U32, name="wb_sb", align_bytes=64)
-        wbs_sb = sb.tile([P, N], U8, name="wbs_sb", align_bytes=64)
+        gate_in = [sb.tile([P, C], F32, name=f"gate_in{h}") for h in range(SLOT_TILES)]
+        w_raw = sb.tile([P, R], U32, name="w_raw", tag="w_raw", align_bytes=MX_ALIGN)
+        ws_raw = sb.tile([P, R], U8, name="ws_raw", align_bytes=MX_ALIGN)
+        wb_sb = sb.tile([P, N], U32, name="wb_sb", align_bytes=MX_ALIGN)
+        wbs_sb = sb.tile([P, N], U8, name="wbs_sb", align_bytes=MX_ALIGN)
         fk_sb = sb.tile([P, PACK], F32, name="fk_sb")
         us_sb = sb.tile([P, PACK], F32, name="us_sb")
-        rs_sb = sb.tile([P, TILES, N], F32, name="rs_sb")
+        rs_sb = sb.tile([P, SLOT_TILES, N], F32, name="rs_sb")
         ident = sb.tile([P, P], F32, name="ident")
 
         warm_in = sb.tile([P, 1], F32, name="warm_in")
@@ -70,68 +82,56 @@ def tile_list_rows_largerpicks_tabled_rowpeaks_kernel(
         nc.sync.dma_start(gate_in[0][:], tg[0:P, :])
         nc.sync.dma_start(fk_sb[:], fk.rearrange("(p t) o -> p (t o)", t=PACK))
         nc.sync.dma_start(gate_in[1][:], tg[P : 2 * P, :])
-        for q in range(4):
-            nc.gpsimd.dma_start(ws_raw[32 * q : 32 * q + 4, :].bitcast(I32), w_scales[0, 4 * q : 4 * q + 4, :].bitcast(I32))
+        load_scale_rows(nc, ws_raw, w_scales[0])
         nc.sync.dma_start(w_raw[:].bitcast(I32), w_words[0].rearrange("p n t -> p (n t)").bitcast(I32))
         nc.sync.dma_start(us_sb[:], us.rearrange("o (p t) -> p (o t)", t=PACK))
         nc.sync.dma_start(rs_sb[:], rs.rearrange("(h p) n -> p h n", p=P))
         nc.sync.dma_start(wb_sb[:].bitcast(I32), wb_words[0].rearrange("p n t -> p (n t)").bitcast(I32))
-        for q in range(4):
-            nc.sync.dma_start(wbs_sb[32 * q : 32 * q + 4, :].bitcast(I32), wb_scales[0, 4 * q : 4 * q + 4, :].bitcast(I32))
+        load_scale_rows(nc, wbs_sb, wb_scales[0])
 
         pick_a = sb.tile([P, PACK, J], F32, name="pick_a")
         pick_b = sb.tile([P, PACK, J], F32, name="pick_b")
         larger = sb.tile([P, PACK, J], F32, name="larger")
-        gate = [sb.tile([P, R], F32, name=f"gate{h}") for h in range(TILES)]
+        gate = [sb.tile([P, R], F32, name=f"gate{h}") for h in range(SLOT_TILES)]
         first_bank = ps.tile([P, PACK, P], F32, name="first_bank", tag="first_bank")
         gate_ps = [
             [first_bank[:, t, :] for t in range(PACK)],
             [ps.tile([P, P], F32, name=f"gate_ps{t}")[:] for t in range(PACK)],
         ]
-        gate_us = [sb.tile([P, PACK, P], F32, name=f"gate_us{h}") for h in range(TILES)]
-        w_sb = sb.tile([P, R], U32, name="w_sb", align_bytes=64)
-        ws_sb = sb.tile([P, R], U8, name="ws_sb", align_bytes=64)
-
-        def gate_gather(h):
-            nc.scalar.activation(gate[h][:], gate_in[h][:].indirect(list_g[:]), ACT.Sigmoid)
-            for t in range(PACK):
-                nc.tensor.transpose(gate_ps[h][t], gate[h][:, t::PACK], ident[:])
-
-        def gate_out(h):
-            for t in range(PACK):
-                nc.scalar.activation(gate_us[h][:, t, :], gate_ps[h][t], ACT.Copy, scale=us_sb[:, t : t + 1])
+        gate_us = [sb.tile([P, PACK, P], F32, name=f"gate_us{h}") for h in range(SLOT_TILES)]
+        w_sb = sb.tile([P, R], U32, name="w_sb", align_bytes=MX_ALIGN)
+        ws_sb = sb.tile([P, R], U8, name="ws_sb", align_bytes=MX_ALIGN)
 
         for t in range(PACK):
             nc.scalar.activation(pick_b[:, t, :], x_plane[t][:].indirect(list_b[:]), ACT.Copy)
             if t < PACK - 1:
                 nc.vector.tensor_copy(pick_a[:, t, :], x_plane[t][:].indirect(list_a[:]))
             else:
-                half = J // 2
-                nc.vector.tensor_copy(pick_a[:, t, :half], x_plane[t][:].indirect(list_a[:, : half // 16]))
-                nc.scalar.activation(pick_a[:, t, half:], x_plane[t][:].indirect(list_a[:, half // 16 :]), ACT.Copy)
+                cut = SHARED_ENTRIES // LIST_ROWS
+                nc.vector.tensor_copy(pick_a[:, t, :SHARED_ENTRIES], x_plane[t][:].indirect(list_a[:, :cut]))
+                nc.scalar.activation(pick_a[:, t, SHARED_ENTRIES:], x_plane[t][:].indirect(list_a[:, cut:]), ACT.Copy)
         for planes in (slice(0, 2), slice(2, 3), slice(3, 4)):
             nc.vector.tensor_tensor(larger[:, planes, :], pick_a[:, planes, :], pick_b[:, planes, :], ALU.max)
-        gate_gather(0)
-        gate_gather(1)
-        gate_out(0)
-        gate_out(1)
 
-        u_bf = [sb.tile([P, P, PACK], BF16, name=f"u_bf{h}", align_bytes=64) for h in range(TILES)]
-        u_q = [sb.tile([P, P], U32, name=f"u_q{h}", align_bytes=64) for h in range(TILES)]
-        u_s = [sb.tile([P, P], U8, name=f"u_s{h}", align_bytes=64) for h in range(TILES)]
-        fk_b = fk_sb[:].unsqueeze(1).unsqueeze(3).to_broadcast([P, P // LINE, PACK, LINE])
-        for h in range(TILES):
-            nc.vector.tensor_tensor(words_by_line(u_bf[h][:]), by_line(larger[:, :, h * P : (h + 1) * P]), fk_b, ALU.mult)
-        nc.vector.tensor_copy(
-            w_sb[:].bitcast(I32).rearrange("p (t c i) -> p c t i", t=PACK, i=4),
-            w_raw[:].bitcast(I32).rearrange("p (c i t) -> p c t i", t=PACK, i=4),
-        )
-        nc.gpsimd.tensor_copy(
-            ws_sb[:].rearrange("p (t m) -> p t m", t=PACK), ws_raw[:].rearrange("p (m t) -> p t m", t=PACK)
-        )
-        a_ps = [ps.tile([P, PACK, P], F32, name=f"a_ps{h}") for h in range(TILES)]
-        for h in range(TILES):
-            nc.vector.quantize_mx(u_q[h][:].bitcast(E5M2X4), u_s[h][:], u_bf[h][:].rearrange("p j t -> p (j t)"))
+        for h in range(SLOT_TILES):
+            nc.scalar.activation(gate[h][:], gate_in[h][:].indirect(list_g[:]), ACT.Sigmoid)
+            for t in range(PACK):
+                nc.tensor.transpose(gate_ps[h][t], gate[h][:, t::PACK], ident[:])
+        for h in range(SLOT_TILES):
+            for t in range(PACK):
+                nc.scalar.activation(gate_us[h][:, t, :], gate_ps[h][t], ACT.Copy, scale=us_sb[:, t : t + 1])
+
+        u_q = [sb.tile([P, P], U32, name=f"u_q{h}", align_bytes=MX_ALIGN) for h in range(SLOT_TILES)]
+        u_s = [sb.tile([P, P], U8, name=f"u_s{h}", align_bytes=MX_ALIGN) for h in range(SLOT_TILES)]
+        a_ps = [ps.tile([P, PACK, P], F32, name=f"a_ps{h}") for h in range(SLOT_TILES)]
+        fk_b = fk_sb[:].unsqueeze(1).unsqueeze(3).to_broadcast([P, P // PAIR, PACK, PAIR])
+
+        def quantise_u(h, u_bf):
+            slots = slice(h * P, (h + 1) * P)
+            nc.vector.tensor_tensor(words_by_pairs(u_bf[:]), planes_by_pairs(larger[:, :, slots]), fk_b, ALU.mult)
+            nc.vector.quantize_mx(u_q[h][:].bitcast(E5M2X4), u_s[h][:], u_bf[:].rearrange("p j t -> p (j t)"))
+
+        def first_product(h):
             for t in range(PACK):
                 nc.tensor.matmul_mx(
                     a_ps[h][:, t, :],
@@ -143,15 +143,29 @@ def tile_list_rows_largerpicks_tabled_rowpeaks_kernel(
                     stop=True,
                 )
 
-        rs3 = sb.tile([P, TILES, N], F32, name="rs3")
-        nc.scalar.activation(rs3[:], rs_sb[:], ACT.Copy, scale=0.3)
+        quantise_u(0, sb.tile([P, P, PACK], BF16, name="u_bf0", align_bytes=MX_ALIGN))
+        nc.vector.tensor_copy(
+            ws_sb[:].rearrange("p (t m) -> p t m", t=PACK), ws_raw[:].rearrange("p (m t) -> p t m", t=PACK)
+        )
+        nc.vector.tensor_copy(
+            w_sb[:].bitcast(I32).rearrange("p (t c i) -> p c t i", t=PACK, i=LINE_WORDS),
+            w_raw[:].bitcast(I32).rearrange("p (c i t) -> p c t i", t=PACK, i=LINE_WORDS),
+        )
+        first_product(0)
+        quantise_u(1, sb.tile([P, P, PACK], BF16, name="u_bf1", tag="w_raw", align_bytes=MX_ALIGN))
+        first_product(1)
 
-        h_bf = [sb.tile([P, P, PACK], BF16, name=f"h_bf{h}", align_bytes=64) for h in range(TILES)]
-        h_q = [sb.tile([P, P], U32, name=f"h_q{h}", align_bytes=64) for h in range(TILES)]
-        h_s = [sb.tile([P, P], U8, name=f"h_s{h}", align_bytes=64) for h in range(TILES)]
+        rs_scaled = sb.tile([P, SLOT_TILES, N], F32, name="rs_scaled")
+        nc.scalar.activation(rs_scaled[:], rs_sb[:], ACT.Copy, scale=0.3)
+
+        h_bf = [sb.tile([P, P, PACK], BF16, name=f"h_bf{h}", align_bytes=MX_ALIGN) for h in range(SLOT_TILES)]
+        h_q = [sb.tile([P, P], U32, name=f"h_q{h}", align_bytes=MX_ALIGN) for h in range(SLOT_TILES)]
+        h_s = [sb.tile([P, P], U8, name=f"h_s{h}", align_bytes=MX_ALIGN) for h in range(SLOT_TILES)]
         p_ps = [ps.tile([P, N], F32, name="p_ps0", tag="first_bank"), ps.tile([P, N], F32, name="p_ps1")]
-        for h in range(TILES):
-            nc.vector.tensor_tensor(words_by_line(h_bf[h][:]), by_line(a_ps[h][:]), by_line(gate_us[h][:]), ALU.mult)
+        for h in range(SLOT_TILES):
+            nc.vector.tensor_tensor(
+                words_by_pairs(h_bf[h][:]), planes_by_pairs(a_ps[h][:]), planes_by_pairs(gate_us[h][:]), ALU.mult
+            )
             nc.vector.quantize_mx(h_q[h][:].bitcast(E5M2X4), h_s[h][:], h_bf[h][:].rearrange("p j t -> p (j t)"))
             nc.tensor.matmul_mx(
                 p_ps[h][:],
@@ -163,14 +177,13 @@ def tile_list_rows_largerpicks_tabled_rowpeaks_kernel(
                 stop=True,
             )
 
-        mag = [sb.tile([P, N], F32, name=f"mag{h}") for h in range(TILES)]
-        mag_up = [sb.tile([P, N], F32, name=f"mag_up{h}") for h in range(TILES)]
-        den = [sb.tile([P, 1], F32, name=f"den{h}") for h in range(TILES)]
-        inv = [sb.tile([P, 1], F32, name=f"inv{h}") for h in range(TILES)]
-        res = [sb.tile([P, N], F32, name=f"res{h}") for h in range(TILES)]
-        for h in range(TILES):
-            nc.scalar.activation(mag[h][:], p_ps[h][:], ACT.Abs)
-            nc.vector.tensor_scalar(mag_up[h][:], mag[h][:], 0.2, None, ALU.add, ALU.max, accum_out=den[h][:])
-            nc.vector.reciprocal(inv[h][:], den[h][:])
-            nc.vector.scalar_tensor_tensor(res[h][:], p_ps[h][:], inv[h][:], rs3[:, h, :], ALU.mult, ALU.add)
-            nc.sync.dma_start(out[h * P : (h + 1) * P, :], res[h][:])
+        for h in range(SLOT_TILES):
+            mag = sb.tile([P, N], F32, name=f"mag{h}")
+            den = sb.tile([P, 1], F32, name=f"den{h}")
+            inv = sb.tile([P, 1], F32, name=f"inv{h}")
+            res = sb.tile([P, N], F32, name=f"res{h}")
+            nc.scalar.activation(mag[:], p_ps[h][:], ACT.Abs)
+            nc.vector.tensor_scalar(mag[:], mag[:], 0.2, None, ALU.add, ALU.max, accum_out=den[:])
+            nc.vector.reciprocal(inv[:], den[:])
+            nc.vector.scalar_tensor_tensor(res[:], p_ps[h][:], inv[:], rs_scaled[:, h, :], ALU.mult, ALU.add)
+            nc.sync.dma_start(out[h * P : (h + 1) * P, :], res[:])

from contextlib import ExitStack

import concourse.mybir as mybir
from concourse.masks import make_identity

K, T, J, R, C, N = 512, 512, 256, 512, 1024, 256
FLOPS = 2 * J * K * R + 2 * J * R * N

F32 = mybir.dt.float32
BF16 = mybir.dt.bfloat16
I32 = mybir.dt.int32
U32 = mybir.dt.uint32
U16 = mybir.dt.uint16
U8 = mybir.dt.uint8
E5M2X4 = mybir.dt.float8_e5m2_x4
E4M3X4 = mybir.dt.float8_e4m3fn_x4
ALU = mybir.AluOpType
ACT = mybir.ActivationFunctionType

P = 128
PACK = 4
SLOT_TILES = J // P
LIST_ROWS = 16
QUADRANTS = 4
MX_ALIGN = 64
PAIR = 2
LINE_WORDS = 4
SHARED_ENTRIES = J // 2


def planes_by_pairs(planes):
    return planes.rearrange("p t (c i) -> p c t i", i=PAIR)


def words_by_pairs(words):
    return words.rearrange("p (c i) t -> p c t i", i=PAIR)


def load_scale_rows(nc, tile, scales):
    for q in range(QUADRANTS):
        nc.sync.dma_start(tile[32 * q : 32 * q + 4, :].bitcast(I32), scales[4 * q : 4 * q + 4, :].bitcast(I32))


def tile_list_rows_largerpicks_tabled_rowpeaks_kernel(
    tc, xf, fk, w_words, w_scales, us, tg, wb_words, wb_scales, rs, offs, offs2, offs3, out
):
    nc = tc.nc
    with ExitStack() as ctx:
        sb = ctx.enter_context(tc.tile_pool(name="sb", bufs=1))
        ps = ctx.enter_context(tc.psum_pool(name="ps", bufs=1))

        list_a = sb.tile([P, J // LIST_ROWS], U16, name="list_a")
        list_b = sb.tile([P, J // LIST_ROWS], U16, name="list_b")
        list_g = sb.tile([P, R // LIST_ROWS], U16, name="list_g")
        x_plane = [sb.tile([P, T], F32, name=f"x_plane{t}") for t in range(PACK)]
        gate_in = [sb.tile([P, C], F32, name=f"gate_in{h}") for h in range(SLOT_TILES)]
        w_raw = sb.tile([P, R], U32, name="w_raw", tag="w_raw", align_bytes=MX_ALIGN)
        ws_raw = sb.tile([P, R], U8, name="ws_raw", align_bytes=MX_ALIGN)
        wb_sb = sb.tile([P, N], U32, name="wb_sb", align_bytes=MX_ALIGN)
        wbs_sb = sb.tile([P, N], U8, name="wbs_sb", align_bytes=MX_ALIGN)
        fk_sb = sb.tile([P, PACK], F32, name="fk_sb")
        us_sb = sb.tile([P, PACK], F32, name="us_sb")
        rs_sb = sb.tile([P, SLOT_TILES, N], F32, name="rs_sb")
        ident = sb.tile([P, P], F32, name="ident")

        warm_in = sb.tile([P, 1], F32, name="warm_in")
        warm_out = sb.tile([P, 1], F32, name="warm_out")
        nc.gpsimd.memset(ws_raw[:].bitcast(I32), 0)
        nc.vector.memset(warm_in[:], 0.0)
        nc.scalar.activation(warm_out[:], warm_in[:], ACT.Sigmoid)
        nc.vector.memset(wbs_sb[:].bitcast(I32), 0)
        nc.vector.memset(ident[:], 0.0)
        make_identity(nc, ident[:], nomemset=True)

        xf_planes = xf.rearrange("(p t) c -> p t c", t=PACK)
        nc.sync.dma_start(x_plane[0][:], xf_planes[:, 0, :])
        nc.sync.dma_start(list_a[:], offs)
        nc.sync.dma_start(list_b[:], offs2)
        for t in range(1, PACK):
            nc.sync.dma_start(x_plane[t][:], xf_planes[:, t, :])
        nc.sync.dma_start(list_g[:], offs3)
        nc.sync.dma_start(gate_in[0][:], tg[0:P, :])
        nc.sync.dma_start(fk_sb[:], fk.rearrange("(p t) o -> p (t o)", t=PACK))
        nc.sync.dma_start(gate_in[1][:], tg[P : 2 * P, :])
        load_scale_rows(nc, ws_raw, w_scales[0])
        nc.sync.dma_start(w_raw[:].bitcast(I32), w_words[0].rearrange("p n t -> p (n t)").bitcast(I32))
        nc.sync.dma_start(us_sb[:], us.rearrange("o (p t) -> p (o t)", t=PACK))
        nc.sync.dma_start(rs_sb[:], rs.rearrange("(h p) n -> p h n", p=P))
        nc.sync.dma_start(wb_sb[:].bitcast(I32), wb_words[0].rearrange("p n t -> p (n t)").bitcast(I32))
        load_scale_rows(nc, wbs_sb, wb_scales[0])

        pick_a = sb.tile([P, PACK, J], F32, name="pick_a")
        pick_b = sb.tile([P, PACK, J], F32, name="pick_b")
        larger = sb.tile([P, PACK, J], F32, name="larger")
        gate = [sb.tile([P, R], F32, name=f"gate{h}") for h in range(SLOT_TILES)]
        first_bank = ps.tile([P, PACK, P], F32, name="first_bank", tag="first_bank")
        gate_ps = [
            [first_bank[:, t, :] for t in range(PACK)],
            [ps.tile([P, P], F32, name=f"gate_ps{t}")[:] for t in range(PACK)],
        ]
        gate_us = [sb.tile([P, PACK, P], F32, name=f"gate_us{h}") for h in range(SLOT_TILES)]
        w_sb = sb.tile([P, R], U32, name="w_sb", align_bytes=MX_ALIGN)
        ws_sb = sb.tile([P, R], U8, name="ws_sb", align_bytes=MX_ALIGN)

        for t in range(PACK):
            nc.scalar.activation(pick_b[:, t, :], x_plane[t][:].indirect(list_b[:]), ACT.Copy)
            if t < PACK - 1:
                nc.vector.tensor_copy(pick_a[:, t, :], x_plane[t][:].indirect(list_a[:]))
            else:
                cut = SHARED_ENTRIES // LIST_ROWS
                nc.vector.tensor_copy(pick_a[:, t, :SHARED_ENTRIES], x_plane[t][:].indirect(list_a[:, :cut]))
                nc.scalar.activation(pick_a[:, t, SHARED_ENTRIES:], x_plane[t][:].indirect(list_a[:, cut:]), ACT.Copy)
        for planes in (slice(0, 2), slice(2, 3), slice(3, 4)):
            nc.vector.tensor_tensor(larger[:, planes, :], pick_a[:, planes, :], pick_b[:, planes, :], ALU.max)

        for h in range(SLOT_TILES):
            nc.scalar.activation(gate[h][:], gate_in[h][:].indirect(list_g[:]), ACT.Sigmoid)
            for t in range(PACK):
                nc.tensor.transpose(gate_ps[h][t], gate[h][:, t::PACK], ident[:])
        for h in range(SLOT_TILES):
            for t in range(PACK):
                nc.scalar.activation(gate_us[h][:, t, :], gate_ps[h][t], ACT.Copy, scale=us_sb[:, t : t + 1])

        u_q = [sb.tile([P, P], U32, name=f"u_q{h}", align_bytes=MX_ALIGN) for h in range(SLOT_TILES)]
        u_s = [sb.tile([P, P], U8, name=f"u_s{h}", align_bytes=MX_ALIGN) for h in range(SLOT_TILES)]
        a_ps = [ps.tile([P, PACK, P], F32, name=f"a_ps{h}") for h in range(SLOT_TILES)]
        fk_b = fk_sb[:].unsqueeze(1).unsqueeze(3).to_broadcast([P, P // PAIR, PACK, PAIR])

        def quantise_u(h, u_bf):
            slots = slice(h * P, (h + 1) * P)
            nc.vector.tensor_tensor(words_by_pairs(u_bf[:]), planes_by_pairs(larger[:, :, slots]), fk_b, ALU.mult)
            nc.vector.quantize_mx(u_q[h][:].bitcast(E5M2X4), u_s[h][:], u_bf[:].rearrange("p j t -> p (j t)"))

        def first_product(h):
            for t in range(PACK):
                nc.tensor.matmul_mx(
                    a_ps[h][:, t, :],
                    lhsT=w_sb[:, t * P : (t + 1) * P].bitcast(E5M2X4),
                    lhsT_scale=ws_sb[:, t * P : (t + 1) * P],
                    rhs=u_q[h][:].bitcast(E5M2X4),
                    rhs_scale=u_s[h][:],
                    start=True,
                    stop=True,
                )

        quantise_u(0, sb.tile([P, P, PACK], BF16, name="u_bf0", align_bytes=MX_ALIGN))
        nc.vector.tensor_copy(
            ws_sb[:].rearrange("p (t m) -> p t m", t=PACK), ws_raw[:].rearrange("p (m t) -> p t m", t=PACK)
        )
        nc.vector.tensor_copy(
            w_sb[:].bitcast(I32).rearrange("p (t c i) -> p c t i", t=PACK, i=LINE_WORDS),
            w_raw[:].bitcast(I32).rearrange("p (c i t) -> p c t i", t=PACK, i=LINE_WORDS),
        )
        first_product(0)
        quantise_u(1, sb.tile([P, P, PACK], BF16, name="u_bf1", tag="w_raw", align_bytes=MX_ALIGN))
        first_product(1)

        rs_scaled = sb.tile([P, SLOT_TILES, N], F32, name="rs_scaled")
        nc.scalar.activation(rs_scaled[:], rs_sb[:], ACT.Copy, scale=0.3)

        h_bf = [sb.tile([P, P, PACK], BF16, name=f"h_bf{h}", align_bytes=MX_ALIGN) for h in range(SLOT_TILES)]
        h_q = [sb.tile([P, P], U32, name=f"h_q{h}", align_bytes=MX_ALIGN) for h in range(SLOT_TILES)]
        h_s = [sb.tile([P, P], U8, name=f"h_s{h}", align_bytes=MX_ALIGN) for h in range(SLOT_TILES)]
        p_ps = [ps.tile([P, N], F32, name="p_ps0", tag="first_bank"), ps.tile([P, N], F32, name="p_ps1")]
        for h in range(SLOT_TILES):
            nc.vector.tensor_tensor(
                words_by_pairs(h_bf[h][:]), planes_by_pairs(a_ps[h][:]), planes_by_pairs(gate_us[h][:]), ALU.mult
            )
            nc.vector.quantize_mx(h_q[h][:].bitcast(E5M2X4), h_s[h][:], h_bf[h][:].rearrange("p j t -> p (j t)"))
            nc.tensor.matmul_mx(
                p_ps[h][:],
                lhsT=h_q[h][:].bitcast(E5M2X4),
                lhsT_scale=h_s[h][:],
                rhs=wb_sb[:].bitcast(E4M3X4),
                rhs_scale=wbs_sb[:],
                start=True,
                stop=True,
            )

        for h in range(SLOT_TILES):
            mag = sb.tile([P, N], F32, name=f"mag{h}")
            den = sb.tile([P, 1], F32, name=f"den{h}")
            inv = sb.tile([P, 1], F32, name=f"inv{h}")
            res = sb.tile([P, N], F32, name=f"res{h}")
            nc.scalar.activation(mag[:], p_ps[h][:], ACT.Abs)
            nc.vector.tensor_scalar(mag[:], mag[:], 0.2, None, ALU.add, ALU.max, accum_out=den[:])
            nc.vector.reciprocal(inv[:], den[:])
            nc.vector.scalar_tensor_tensor(res[:], p_ps[h][:], inv[:], rs_scaled[:, h, :], ALU.mult, ALU.add)
            nc.sync.dma_start(out[h * P : (h + 1) * P, :], res[:])
